import numpy as np
import ml_dtypes


def mxq(x, axis, fmt="e4m3"):
    dtype, down = {"e4m3": (ml_dtypes.float8_e4m3fn, 7), "e5m2": (ml_dtypes.float8_e5m2, 14)}[fmt]
    v = np.moveaxis(np.asarray(x, np.float32).astype(ml_dtypes.bfloat16).astype(np.float64), axis, -1)
    blocks = v.reshape(v.shape[:-1] + (-1, 32))
    amax = np.abs(blocks).max(-1, keepdims=True)
    byte = np.maximum(np.where(amax > 0, np.frexp(amax)[1] - 1 + 127, 0) - down, 1)
    scale = np.exp2(byte - 127.0)
    codes = (blocks / scale).astype(np.float32).astype(dtype).astype(np.float64)
    return np.moveaxis((codes * scale).reshape(v.shape), -1, axis)


WIDE = False


def mx_kscale(k):
    if not WIDE:
        return np.ones(k)
    levels = np.array([10, -10, 5, -5, 0])
    if k % 512:
        return np.exp2(np.random.permutation(np.resize(levels, k // 32))).repeat(32)
    a = np.empty((k // 512, 16))
    for p in range(k // 512):
        a[p, :8] = np.random.permutation(np.resize(levels, 8))
        for g in range(8):
            far = levels[np.abs(levels - a[p, g]) >= 10]
            a[p, g + 8] = far[np.random.randint(len(far))]
    return np.exp2(a.ravel()).repeat(32)


BF16 = ml_dtypes.bfloat16


def bf(x):
    return np.asarray(x, np.float32).astype(BF16)


def f64(x):
    return np.asarray(x).astype(np.float64)


E2M1 = np.array([0.0, 0.5, 1.0, 1.5, 2.0, 3.0, 4.0, 6.0, -0.0, -0.5, -1.0, -1.5, -2.0, -3.0, -4.0, -6.0])


def pack_weight(w, fmt):
    k, n = w.shape
    w = f64(bf(w)).reshape(k // 32, 32, n)
    amax = np.abs(w).max(1)
    if fmt == "e4m3":
        byte = np.frexp(amax)[1] - 1 + 127 - 7
    else:
        mant, ex = np.frexp(amax / 6.0)
        byte = np.where(mant > 0.5, ex, ex - 1) + 127
    byte = np.clip(np.where(amax > 0, byte, 1), 1, 254)
    scaled = (w * np.exp2(127.0 - byte)[:, None, :]).reshape(k, n).astype(np.float32)
    by_word = np.ascontiguousarray(scaled.reshape(k // 512, 128, 4, n).transpose(0, 1, 3, 2))
    if fmt == "e4m3":
        words = by_word.astype(ml_dtypes.float8_e4m3fn).view(np.uint8)
    else:
        c = by_word.astype(ml_dtypes.float4_e2m1fn).view(np.uint8) & 0xF
        words = c[..., 0::2] | (c[..., 1::2] << 4)
    return np.ascontiguousarray(words), np.ascontiguousarray(byte.astype(np.uint8).reshape(k // 512, 16, n))


def unpack_weight(words, scales, fmt):
    g, p, n, _ = words.shape
    if fmt == "e4m3":
        vals = np.ascontiguousarray(words).view(ml_dtypes.float8_e4m3fn).astype(np.float64)
    else:
        nib = np.empty((g, p, n, 4), np.uint8)
        nib[..., 0::2] = words & 0xF
        nib[..., 1::2] = words >> 4
        vals = E2M1[nib]
    vals = vals * np.repeat(np.exp2(scales.astype(np.float64) - 127.0), 8, axis=1)[..., None]
    return vals.transpose(0, 1, 3, 2).reshape(g * 512, n)
def pack4(w):
    words, scales = pack_weight(w, "e2m1")
    return words.reshape(words.shape[0], 128, -1), scales


def unpack4(words, scales):
    return unpack_weight(words.reshape(words.shape[0], 128, -1, 2), scales, "e2m1")


def planes(Y):
    n, m = Y.shape
    b = f64(bf(Y)).reshape(n // 32, 32, m)
    amax = np.abs(b).max(1)
    byte = np.clip(np.where(amax > 0, np.frexp(amax)[1] - 1 + 127 - 7, 1), 1, 254)
    codes = (b * np.exp2(127.0 - byte)[:, None, :]).reshape(n, m).astype(np.float32).astype(ml_dtypes.float8_e4m3fn).view(np.uint8)
    words = codes.reshape(n // 512, 128, 4, m).transpose(0, 1, 3, 2)
    return np.ascontiguousarray(words), np.ascontiguousarray(byte.astype(np.uint8).reshape(n // 512, 16, m))


P, B, R = 2048, 1024, 512


def setup_inputs():
    s = mx_kscale(B)
    t = mx_kscale(R)
    x = bf(np.random.randn(P, B) * s)
    u = np.random.randn(B, R) / np.sqrt(B) * t / s[:, None]
    u_words, u_scales = pack4(u)
    d = np.random.randn(R, B) * 1.4 / np.sqrt(R) / t[:, None]
    d_words, d_scales = pack4(d)
    bias = bf(0.4 * np.random.randn(R) * t)
    gain = bf((1.0 + 0.1 * np.random.randn(B)) / s)
    weight = bf(np.exp(0.8 * np.random.randn(B)))
    return {"x": x, "u_words": u_words, "u_scales": u_scales, "bias": bias,
            "d_words": d_words, "d_scales": d_scales, "gain": gain, "weight": weight}

def reference(x, u_words, u_scales, bias, d_words, d_scales, gain, weight):
    X = f64(x)
    A = mxq(X, 1, "e4m3") @ unpack4(u_words, u_scales)
    A = np.maximum(A + f64(bias), 0.0)
    fit = mxq(A, 1, "e4m3") @ unpack4(d_words, d_scales)
    y = (X * f64(gain) - fit) * f64(weight)
    Y = y.T
    words, scales = planes(Y)
    return y, words, scales

@@ -1,0 +1,394 @@
+from contextlib import ExitStack
+
+import concourse.mybir as mybir
+from concourse.masks import make_identity
+
+PIXELS, BANDS, MEMBERS = 2048, 1024, 512
+FLOPS = 2 * 2 * PIXELS * BANDS * MEMBERS
+
+F32 = mybir.dt.float32
+BF16 = mybir.dt.bfloat16
+U32 = mybir.dt.uint32
+I32 = mybir.dt.int32
+U8 = mybir.dt.uint8
+FP8X4 = mybir.dt.float8_e4m3fn_x4
+FP4X4 = mybir.dt.float4_e2m1fn_x4
+ALU = mybir.AluOpType
+ACT = mybir.ActivationFunctionType
+
+P = 128
+PACK = 4
+K_PASS = P * PACK
+HALVES = BANDS // K_PASS
+WIDTHS = [512, 512, 512, 512]
+FIT_BANKS = 4
+OTHER_BANKS = 4
+HEAD_S = 2
+HEAD_V = 2
+D_ON_V = [1, 2, 1, 2, 1, 1, 0, 0]
+D_EARLY = [2, 1, 2, 2, 2, 1, 0, 0]
+E_ON_S = [0, 0, 0, 0, 0, 0, 0, 0]
+FIT_EARLY = [2, 2, 2, 2, 2, 3, 3, 0]
+G_COLS = [0, 0, 0, 0, 0, 0, 0, 0]
+YI_BUFS = 2
+
+
+def tile_unmixing_residual_planes_h1_kernel(
+    tc, x, u_words, u_scales, bias, d_words, d_scales, gain, weight, out_0, out_1, out_2
+):
+    nc = tc.nc
+    starts = [sum(WIDTHS[:i]) for i in range(len(WIDTHS))]
+    groups = len(WIDTHS)
+
+    with ExitStack() as ctx:
+        keep = ctx.enter_context(tc.tile_pool(name="keep", bufs=1))
+        work = ctx.enter_context(tc.tile_pool(name="work", bufs=2))
+        psum = ctx.enter_context(tc.psum_pool(name="psum", bufs=1))
+        ctx.enter_context(tc.manual_schedule())
+
+        uw_raw = keep.tile([P, HALVES, 2 * K_PASS], U8, name="uw_raw")
+        dw_raw = keep.tile([P, HALVES, 2 * K_PASS], U8, name="dw_raw")
+        us_raw = keep.tile([P, HALVES, K_PASS], U8, name="us_raw")
+        ds_raw = keep.tile([P, HALVES, K_PASS], U8, name="ds_raw")
+        uw = keep.tile([P, HALVES, 2 * K_PASS], U8, name="uw", align_bytes=64)
+        dw = keep.tile([P, HALVES, 2 * K_PASS], U8, name="dw", align_bytes=64)
+        us = keep.tile([P, HALVES, K_PASS], U8, name="us", align_bytes=64)
+        ds = keep.tile([P, HALVES, K_PASS], U8, name="ds", align_bytes=64)
+        bias_sb = keep.tile([P, PACK], BF16, name="bias_sb")
+        gain_sb = keep.tile([P, HALVES, PACK], BF16, name="gain_sb")
+        weight_sb = keep.tile([P, HALVES, PACK], BF16, name="weight_sb")
+        gw = keep.tile([P, HALVES, PACK], F32, name="gw")
+        neg_w = keep.tile([P, HALVES, PACK], F32, name="neg_w")
+        ident = keep.tile([P, P], F32, name="ident")
+        y_codes = keep.tile([P, HALVES, PIXELS], U32, name="y_codes", align_bytes=64)
+        y_scales = keep.tile([P, HALVES, PIXELS], U8, name="y_scales", align_bytes=64)
+
+        x_view = x.rearrange("(j p) b -> p j b", p=P)
+
+        x_sb = {}
+
+        def load_x(j0, j1, g0=0, g1=HALVES):
+            part = keep.tile([P, j1 - j0, K_PASS * (g1 - g0)], BF16, name="x_%d_%d" % (j0, g0))
+            nc.sync.dma_start(out=part[:], in_=x_view[:, j0:j1, K_PASS * g0 : K_PASS * g1])
+            for j in range(j0, j1):
+                for g in range(g0, g1):
+                    x_sb[j, g] = part[:, j - j0, K_PASS * (g - g0) : K_PASS * (g - g0 + 1)]
+
+        def load_scales(queue, raw, rows):
+            for q in range(4):
+                queue.dma_start(out=raw[32 * q : 32 * q + 4].bitcast(I32), in_=rows[4 * q : 4 * q + 4].bitcast(I32))
+
+        def permute_words(dst, raw, g):
+            nc.vector.tensor_copy(
+                out=dst[:, g, :].rearrange("p (t m b) -> p t m b", t=PACK, b=2),
+                in_=raw[:, g, :].rearrange("p (m t b) -> p t m b", t=PACK, b=2),
+            )
+
+        def permute_scales(dst, raw):
+            nc.vector.tensor_copy(
+                out=dst[:].rearrange("p g (t m) -> p g t m", t=PACK),
+                in_=raw[:].rearrange("p g (m t) -> p g t m", t=PACK),
+            )
+
+        count = {"fit": 0, "other": 0}
+
+        def bank(ring, shape):
+            size = FIT_BANKS if ring == "fit" else OTHER_BANKS
+            tag = "%s%d" % (ring, count[ring] % size)
+            count[ring] = count[ring] + 1
+            return psum.tile(shape, F32, name=tag, tag=tag)
+
+        held = {}
+
+        def tiles(i):
+            return WIDTHS[i] // P
+
+        def pairs(i):
+            return (tiles(i) + 1) // 2
+
+        def copier(eng):
+            return nc.vector.tensor_copy if eng == "V" else nc.scalar.copy
+
+        def turn_x(i, g, pair):
+            n = min(2, tiles(i) - 2 * pair)
+            b = bank("other", [P, 2, 2, P])
+            for jj in range(n):
+                words = x_sb[starts[i] // P + 2 * pair + jj, g].bitcast(F32)
+                for u in range(2):
+                    nc.tensor.transpose(b[:, jj, u, :], words[:, u::2], ident[:])
+            held["xb", i, g, pair] = b
+
+        def copy_x(i, g, pair, eng="S"):
+            n = min(2, tiles(i) - 2 * pair)
+            if pair == 0:
+                held["xt", i, g] = work.tile([P, WIDTHS[i], PACK], BF16, name="xt%d" % g, align_bytes=64)
+            words = held["xt", i, g][:].rearrange("p m t -> p (m t)").bitcast(F32)
+            copier(eng)(
+                out=words[:, 512 * pair : 512 * pair + 256 * n].rearrange("p (j m u) -> p j m u", j=n, u=2),
+                in_=held["xb", i, g, pair][:, 0:n].rearrange("p j u m -> p j m u"),
+            )
+
+        def quantise_x(i, g):
+            codes = work.tile([P, WIDTHS[i]], U32, name="xq%d" % g, align_bytes=64)
+            scales = work.tile([P, WIDTHS[i]], U8, name="xs%d" % g, align_bytes=64)
+            nc.vector.quantize_mx(
+                out=codes[:].bitcast(FP8X4), scales=scales[:], in_=held["xt", i, g][:].rearrange("p m t -> p (m t)")
+            )
+            held["xq", i, g] = (codes, scales)
+
+        def scale_x(i, g, t, eng):
+            if ("y", i, g) not in held:
+                held["y", i, g] = work.tile([P, PACK, WIDTHS[i]], F32, name="y%d" % g, bufs=2)
+            dst = held["y", i, g][:, t, :]
+            src = held["xt", i, g][:, :, t]
+            if eng == "V":
+                nc.vector.tensor_scalar(out=dst, in0=src, scalar1=gw[:, g, t : t + 1], scalar2=None, op0=ALU.mult)
+            else:
+                nc.scalar.activation(out=dst, in_=src, func=ACT.Copy, scale=gw[:, g, t : t + 1])
+
+        def unmix(i, t):
+            w = WIDTHS[i]
+            b = bank("other", [P, w])
+            n = w if w == 512 else P
+            for m0 in range(0, w, n):
+                for g in range(HALVES):
+                    codes, scales = held["xq", i, g]
+                    nc.tensor.matmul_mx(
+                        out=b[:, m0 : m0 + n],
+                        lhsT=uw[:, g, 256 * t : 256 * (t + 1)].bitcast(FP4X4),
+                        lhsT_scale=us[:, g, P * t : P * (t + 1)],
+                        rhs=codes[:, m0 : m0 + n].bitcast(FP8X4),
+                        rhs_scale=scales[:, m0 : m0 + n],
+                        start=(g == 0),
+                        stop=(g == HALVES - 1),
+                    )
+            held["ab", i, t] = b
+
+        def relu(i, t, eng="S"):
+            if t == 0:
+                held["a", i] = work.tile([P, PACK, WIDTHS[i]], BF16, name="a", bufs=1)
+            nc.scalar.activation(out=held["a", i][:, t, :], in_=held["ab", i, t][:], func=ACT.Relu, bias=bias_sb[:, t : t + 1])
+
+        def interleave(dst, src, eng):
+            copier(eng)(
+                out=dst.rearrange("p (c i) t -> p c t i", i=4), in_=src.rearrange("p t (c i) -> p c t i", i=4)
+            )
+
+        def interleave_a(i, eng="V"):
+            held["ai", i] = work.tile([P, WIDTHS[i], PACK], BF16, name="ai", bufs=1, align_bytes=64)
+            interleave(held["ai", i][:], held["a", i][:], eng)
+
+        def quantise_a(i):
+            codes = work.tile([P, WIDTHS[i]], U32, name="aq", align_bytes=64)
+            scales = work.tile([P, WIDTHS[i]], U8, name="asc", align_bytes=64)
+            nc.vector.quantize_mx(
+                out=codes[:].bitcast(FP8X4), scales=scales[:], in_=held["ai", i][:].rearrange("p m t -> p (m t)")
+            )
+            held["aq", i] = (codes, scales)
+
+        def rebuild(i, g, t):
+            b = bank("fit", [P, WIDTHS[i]])
+            codes, scales = held["aq", i]
+            nc.tensor.matmul_mx(
+                out=b[:],
+                lhsT=dw[:, g, 256 * t : 256 * (t + 1)].bitcast(FP4X4),
+                lhsT_scale=ds[:, g, P * t : P * (t + 1)],
+                rhs=codes[:].bitcast(FP8X4),
+                rhs_scale=scales[:],
+                start=True,
+                stop=True,
+            )
+            held["fb", i, g, t] = b
+
+        def residual(i, g, t, m0=0, m1=512):
+            y = held["y", i, g][:, t, m0:m1]
+            nc.vector.scalar_tensor_tensor(
+                out=y, in0=held["fb", i, g, t][:, m0:m1], scalar=neg_w[:, g, t : t + 1], in1=y, op0=ALU.mult, op1=ALU.add
+            )
+
+        def turn_y(i, g, j):
+            b = bank("other", [P, PACK, P])
+            for t in range(PACK):
+                nc.tensor.transpose(b[:, t, :], held["y", i, g][:, t, P * j : P * (j + 1)], ident[:])
+            held["yb", i, g, j] = b
+
+        def copy_y(i, g, j, eng="S"):
+            if j == 0:
+                held["yo", i, g] = work.tile([P, tiles(i), K_PASS], F32, name="yo", bufs=3)
+            copier(eng)(
+                out=held["yo", i, g][:, j, :].rearrange("m (p t) -> m p t", t=PACK),
+                in_=held["yb", i, g, j][:].rearrange("m t p -> m p t"),
+            )
+
+        def store_y(i, g, j0, j1):
+            rows = out_0[starts[i] : starts[i] + WIDTHS[i], K_PASS * g : K_PASS * (g + 1)].rearrange("(j m) b -> m j b", m=P)
+            nc.sync.dma_start(out=rows[:, j0:j1, :], in_=held["yo", i, g][:, j0:j1, :])
+
+        def round_y(i, g, m0, m1, eng="V"):
+            if ("yi", i, g) not in held:
+                held["yi", i, g] = work.tile([P, WIDTHS[i], PACK], BF16, name="yi", align_bytes=64, bufs=YI_BUFS)
+            dst = held["yi", i, g][:, m0:m1, :]
+            src = held["y", i, g][:, :, m0:m1]
+            if eng == "G":
+                nc.gpsimd.tensor_scalar(
+                    out=dst, in0=src.rearrange("p t m -> p m t"), scalar1=1.0, scalar2=1.0, op0=ALU.mult, op1=ALU.mult
+                )
+            else:
+                interleave(dst, src, eng)
+
+        def quantise_y(i, g, m0=0, m1=512):
+            cols = slice(starts[i] + m0, starts[i] + m1)
+            nc.vector.quantize_mx(
+                out=y_codes[:, g, cols].bitcast(FP8X4),
+                scales=y_scales[:, g, cols],
+                in_=held["yi", i, g][:, m0:m1, :].rearrange("p m t -> p (m t)"),
+            )
+            words = out_1[g].rearrange("p m t -> p (m t)").bitcast(I32)
+            nc.sync.dma_start(out=words[:, cols], in_=y_codes[:, g, cols].bitcast(I32))
+
+        def store_scales(m0, m1):
+            rows = out_2.rearrange("g q m -> q g m")
+            for q in range(4):
+                nc.sync.dma_start(
+                    out=rows[4 * q : 4 * q + 4, :, m0:m1].bitcast(I32),
+                    in_=y_scales[32 * q : 32 * q + 4, :, m0:m1].bitcast(I32),
+                )
+
+        def scale_some(i, g, ts, eng):
+            for t in ts:
+                scale_x(i, g, t, eng)
+
+        nc.vector.memset(us_raw[:].rearrange("p g n -> p (g n)").bitcast(I32), 0)
+        nc.vector.memset(ds_raw[:].rearrange("p g n -> p (g n)").bitcast(I32), 0)
+        make_identity(nc, ident[:])
+        load_x(0, 2, 0, 1)
+        nc.scalar.dma_start(out=weight_sb[:], in_=weight.rearrange("(g p t) -> p g t", p=P, t=PACK))
+        load_x(2, 4, 0, 1)
+        nc.sync.dma_start(out=uw_raw[:].bitcast(I32), in_=u_words.rearrange("g p n -> p g n").bitcast(I32))
+        load_scales(nc.scalar, us_raw, u_scales.rearrange("g q n -> q g n"))
+        load_x(0, 4, 1, 2)
+        nc.sync.dma_start(out=gain_sb[:], in_=gain.rearrange("(g p t) -> p g t", p=P, t=PACK))
+        nc.sync.dma_start(
+            out=dw_raw[:].rearrange("p g n -> p (g n)").bitcast(I32), in_=d_words[0].bitcast(I32)
+        )
+        load_scales(nc.gpsimd, ds_raw, d_scales[0].rearrange("q (g n) -> q g n", g=HALVES))
+        nc.sync.dma_start(out=bias_sb[:], in_=bias.rearrange("(p t) -> p t", t=PACK))
+        load_x(4, 8)
+        for j0 in range(8, PIXELS // P, 4):
+            load_x(j0, j0 + 4)
+        nc.scalar.activation(out=neg_w[:], in_=weight_sb[:], func=ACT.Copy, scale=-1.0)
+
+        def turn_and_copy_x(i, g):
+            for pair in range(pairs(i)):
+                turn_x(i, g, pair)
+                copy_x(i, g, pair)
+
+        def unmix_all(i):
+            for t in range(PACK):
+                unmix(i, t)
+                relu(i, t)
+
+        turn_and_copy_x(0, 0)
+        turn_and_copy_x(0, 1)
+        for g in range(HALVES):
+            permute_words(uw, uw_raw, g)
+        quantise_x(0, 0)
+        permute_scales(us, us_raw)
+        nc.vector.tensor_tensor(out=gw[:], in0=gain_sb[:], in1=weight_sb[:], op=ALU.mult)
+        quantise_x(0, 1)
+        scale_some(0, 0, range(HEAD_S), "S")
+        unmix_all(0)
+        for g in range(HALVES):
+            permute_words(dw, dw_raw, g)
+        permute_scales(ds, ds_raw)
+        scale_some(0, 0, range(HEAD_S, PACK), "V")
+        turn_and_copy_x(1, 0)
+        turn_and_copy_x(1, 1)
+        scale_some(0, 1, range(HEAD_V), "V")
+        interleave_a(0)
+        quantise_x(1, 0)
+        quantise_a(0)
+        quantise_x(1, 1)
+        scale_some(0, 1, range(HEAD_V, PACK), "S")
+        for t in range(PACK):
+            rebuild(0, 0, t)
+
+        halves = HALVES * groups
+
+        def step(h):
+            i, g = divmod(h, HALVES)
+            n = i + 1
+            last = h == halves - 1
+            on_v = D_ON_V[h]
+            early = D_EARLY[h]
+            before = divmod(h - 1, HALVES)
+            cut = G_COLS[h - 1] if h >= 1 else 0
+            if h >= 2 and G_COLS[h - 2]:
+                quantise_y(*divmod(h - 2, HALVES))
+            if cut:
+                round_y(*before, 0, cut, "G")
+            if h >= 1 and E_ON_S[h - 1]:
+                round_y(*before, 0, E_ON_S[h - 1], "S")
+            if g == 0 and n < groups:
+                unmix_all(n)
+            if g == 1 and n + 1 < groups:
+                turn_and_copy_x(n + 1, 0)
+                turn_and_copy_x(n + 1, 1)
+            if last:
+                for m0 in (0, 256):
+                    for t in range(PACK):
+                        residual(i, g, t, m0, m0 + 256)
+                    if m0 == 0:
+                        if cut and cut < 512:
+                            round_y(*before, cut, 512)
+                        if not cut:
+                            quantise_y(*before)
+                    for j in (m0 // P, m0 // P + 1):
+                        turn_y(i, g, j)
+                        copy_y(i, g, j)
+                        store_y(i, g, j, j + 1)
+                round_y(i, g, 0, 256)
+                if cut:
+                    quantise_y(*before)
+                round_y(i, g, 256, 512)
+                quantise_y(i, g)
+                store_scales(starts[i], PIXELS)
+                return
+            for t in range(PACK):
+                residual(i, g, t)
+            if cut and cut < 512:
+                round_y(*before, cut, 512)
+            if h >= 1 and not cut:
+                quantise_y(*before)
+            if h == halves - 2:
+                store_scales(0, starts[i])
+            if n < groups:
+                scale_some(n, g, range(on_v, on_v + early), "S")
+            s_cols = E_ON_S[h]
+            for t in range(FIT_EARLY[h]):
+                rebuild(*divmod(h + 1, HALVES), t)
+            for j in range(tiles(i)):
+                turn_y(i, g, j)
+                if j == 1:
+                    for t in range(FIT_EARLY[h], PACK):
+                        rebuild(*divmod(h + 1, HALVES), t)
+                copy_y(i, g, j)
+                if j % 2:
+                    store_y(i, g, j - 1, j + 1)
+            if n < groups:
+                scale_some(n, g, range(on_v + early, PACK), "S")
+            if not G_COLS[h] and s_cols < 512:
+                round_y(i, g, s_cols, 512)
+            if g == 0 and n < groups:
+                interleave_a(n)
+            if g == 1 and n + 1 < groups:
+                quantise_x(n + 1, 0)
+            if n < groups:
+                scale_some(n, g, range(on_v), "V")
+            if g == 0 and n < groups:
+                quantise_a(n)
+            if g == 1 and n + 1 < groups:
+                quantise_x(n + 1, 1)
+
+        for h in range(halves):
+            step(h)

@@ -19,26 +19,26 @@ ACT = mybir.ActivationFunctionType
 P = 128
 PACK = 4
 K_PASS = P * PACK
-HALVES = BANDS // K_PASS
-WIDTHS = [512, 512, 512, 512]
-FIT_BANKS = 4
-OTHER_BANKS = 4
-HEAD_S = 2
-HEAD_V = 2
-D_ON_V = [1, 2, 1, 2, 1, 1, 0, 0]
-D_EARLY = [2, 1, 2, 2, 2, 1, 0, 0]
-E_ON_S = [0, 0, 0, 0, 0, 0, 0, 0]
-FIT_EARLY = [2, 2, 2, 2, 2, 3, 3, 0]
-G_COLS = [0, 0, 0, 0, 0, 0, 0, 0]
-YI_BUFS = 2
+G = BANDS // K_PASS
+WIDTH = 512
+TILES = WIDTH // P
+GROUPS = PIXELS // WIDTH
+HALVES = G * GROUPS
+RING = 4
+TURN_AHEAD = 5
+UNMIX_AHEAD = 3
+
+RELU_ON_VECTOR = (2, 4)
+SCALE_ON_VECTOR = [2, 1, 2, 1, 0, 1, 1]
+SCALE_ON_SCALAR = [1, 2, 3, 1, 4, 4, 1]
+ROUND_ON_GPSIMD = [0, 0, 512, 384, 512, 384, 384]
+SCALE_BEFORE_TURN = 3
 
 
 def tile_unmixing_residual_planes_h1_kernel(
     tc, x, u_words, u_scales, bias, d_words, d_scales, gain, weight, out_0, out_1, out_2
 ):
     nc = tc.nc
-    starts = [sum(WIDTHS[:i]) for i in range(len(WIDTHS))]
-    groups = len(WIDTHS)
 
     with ExitStack() as ctx:
         keep = ctx.enter_context(tc.tile_pool(name="keep", bufs=1))
@@ -46,349 +46,328 @@ def tile_unmixing_residual_planes_h1_kernel(
         psum = ctx.enter_context(tc.psum_pool(name="psum", bufs=1))
         ctx.enter_context(tc.manual_schedule())
 
-        uw_raw = keep.tile([P, HALVES, 2 * K_PASS], U8, name="uw_raw")
-        dw_raw = keep.tile([P, HALVES, 2 * K_PASS], U8, name="dw_raw")
-        us_raw = keep.tile([P, HALVES, K_PASS], U8, name="us_raw")
-        ds_raw = keep.tile([P, HALVES, K_PASS], U8, name="ds_raw")
-        uw = keep.tile([P, HALVES, 2 * K_PASS], U8, name="uw", align_bytes=64)
-        dw = keep.tile([P, HALVES, 2 * K_PASS], U8, name="dw", align_bytes=64)
-        us = keep.tile([P, HALVES, K_PASS], U8, name="us", align_bytes=64)
-        ds = keep.tile([P, HALVES, K_PASS], U8, name="ds", align_bytes=64)
+        uw_raw = keep.tile([P, G, 2 * K_PASS], U8, name="uw_raw")
+        dw_raw = keep.tile([P, G, 2 * K_PASS], U8, name="dw_raw")
+        us_raw = keep.tile([P, G, K_PASS], U8, name="us_raw")
+        ds_raw = keep.tile([P, G, K_PASS], U8, name="ds_raw")
+        uw = keep.tile([P, G, 2 * K_PASS], U8, name="uw", align_bytes=64)
+        dw = keep.tile([P, G, 2 * K_PASS], U8, name="dw", align_bytes=64)
+        us = keep.tile([P, G, K_PASS], U8, name="us", align_bytes=64)
+        ds = keep.tile([P, G, K_PASS], U8, name="ds", align_bytes=64)
         bias_sb = keep.tile([P, PACK], BF16, name="bias_sb")
-        gain_sb = keep.tile([P, HALVES, PACK], BF16, name="gain_sb")
-        weight_sb = keep.tile([P, HALVES, PACK], BF16, name="weight_sb")
-        gw = keep.tile([P, HALVES, PACK], F32, name="gw")
-        neg_w = keep.tile([P, HALVES, PACK], F32, name="neg_w")
+        gain_sb = keep.tile([P, G, PACK], BF16, name="gain_sb")
+        weight_sb = keep.tile([P, G, PACK], BF16, name="weight_sb")
+        gain_weight = keep.tile([P, G, PACK], F32, name="gain_weight")
+        neg_weight = keep.tile([P, G, PACK], F32, name="neg_weight")
         ident = keep.tile([P, P], F32, name="ident")
-        y_codes = keep.tile([P, HALVES, PIXELS], U32, name="y_codes", align_bytes=64)
-        y_scales = keep.tile([P, HALVES, PIXELS], U8, name="y_scales", align_bytes=64)
+        main_pixels = PIXELS - WIDTH
+        y_codes = keep.tile([P, G, PIXELS], U32, name="y_codes", align_bytes=64)
+        ys_main = keep.tile([P, G, main_pixels], U8, name="ys_main", align_bytes=64)
+        ys_last = keep.tile([P, G, WIDTH], U8, name="ys_last", align_bytes=64)
 
-        x_view = x.rearrange("(j p) b -> p j b", p=P)
-
+        x_rows = x.rearrange("(j p) b -> p j b", p=P)
         x_sb = {}
+        held = {}
+        used = {"fit": 0, "other": 0}
 
-        def load_x(j0, j1, g0=0, g1=HALVES):
+        def bank(ring, shape):
+            tag = "%s%d" % (ring, used[ring] % RING)
+            used[ring] = used[ring] + 1
+            return psum.tile(shape, F32, name=tag, tag=tag)
+
+        def load_x(j0, j1, g0, g1):
             part = keep.tile([P, j1 - j0, K_PASS * (g1 - g0)], BF16, name="x_%d_%d" % (j0, g0))
-            nc.sync.dma_start(out=part[:], in_=x_view[:, j0:j1, K_PASS * g0 : K_PASS * g1])
+            nc.sync.dma_start(out=part[:], in_=x_rows[:, j0:j1, K_PASS * g0 : K_PASS * g1])
             for j in range(j0, j1):
                 for g in range(g0, g1):
                     x_sb[j, g] = part[:, j - j0, K_PASS * (g - g0) : K_PASS * (g - g0 + 1)]
 
-        def load_scales(queue, raw, rows):
+        def load_scales(raw, rows):
             for q in range(4):
-                queue.dma_start(out=raw[32 * q : 32 * q + 4].bitcast(I32), in_=rows[4 * q : 4 * q + 4].bitcast(I32))
+                nc.sync.dma_start(out=raw[32 * q : 32 * q + 4].bitcast(I32), in_=rows[4 * q : 4 * q + 4].bitcast(I32))
 
-        def permute_words(dst, raw, g):
+        def reorder_words(dst, raw, g):
             nc.vector.tensor_copy(
                 out=dst[:, g, :].rearrange("p (t m b) -> p t m b", t=PACK, b=2),
                 in_=raw[:, g, :].rearrange("p (m t b) -> p t m b", t=PACK, b=2),
             )
 
-        def permute_scales(dst, raw):
+        def reorder_scales(dst, raw):
             nc.vector.tensor_copy(
                 out=dst[:].rearrange("p g (t m) -> p g t m", t=PACK),
                 in_=raw[:].rearrange("p g (m t) -> p g t m", t=PACK),
             )
 
-        count = {"fit": 0, "other": 0}
+        def quantise(codes, scales, values):
+            nc.vector.quantize_mx(out=codes.bitcast(FP8X4), scales=scales, in_=values.rearrange("p m t -> p (m t)"))
 
-        def bank(ring, shape):
-            size = FIT_BANKS if ring == "fit" else OTHER_BANKS
-            tag = "%s%d" % (ring, count[ring] % size)
-            count[ring] = count[ring] + 1
-            return psum.tile(shape, F32, name=tag, tag=tag)
-
-        held = {}
-
-        def tiles(i):
-            return WIDTHS[i] // P
-
-        def pairs(i):
-            return (tiles(i) + 1) // 2
-
-        def copier(eng):
-            return nc.vector.tensor_copy if eng == "V" else nc.scalar.copy
-
-        def turn_x(i, g, pair):
-            n = min(2, tiles(i) - 2 * pair)
-            b = bank("other", [P, 2, 2, P])
-            for jj in range(n):
-                words = x_sb[starts[i] // P + 2 * pair + jj, g].bitcast(F32)
-                for u in range(2):
-                    nc.tensor.transpose(b[:, jj, u, :], words[:, u::2], ident[:])
-            held["xb", i, g, pair] = b
-
-        def copy_x(i, g, pair, eng="S"):
-            n = min(2, tiles(i) - 2 * pair)
-            if pair == 0:
-                held["xt", i, g] = work.tile([P, WIDTHS[i], PACK], BF16, name="xt%d" % g, align_bytes=64)
-            words = held["xt", i, g][:].rearrange("p m t -> p (m t)").bitcast(F32)
-            copier(eng)(
-                out=words[:, 512 * pair : 512 * pair + 256 * n].rearrange("p (j m u) -> p j m u", j=n, u=2),
-                in_=held["xb", i, g, pair][:, 0:n].rearrange("p j u m -> p j m u"),
-            )
-
-        def quantise_x(i, g):
-            codes = work.tile([P, WIDTHS[i]], U32, name="xq%d" % g, align_bytes=64)
-            scales = work.tile([P, WIDTHS[i]], U8, name="xs%d" % g, align_bytes=64)
-            nc.vector.quantize_mx(
-                out=codes[:].bitcast(FP8X4), scales=scales[:], in_=held["xt", i, g][:].rearrange("p m t -> p (m t)")
-            )
-            held["xq", i, g] = (codes, scales)
-
-        def scale_x(i, g, t, eng):
-            if ("y", i, g) not in held:
-                held["y", i, g] = work.tile([P, PACK, WIDTHS[i]], F32, name="y%d" % g, bufs=2)
-            dst = held["y", i, g][:, t, :]
-            src = held["xt", i, g][:, :, t]
-            if eng == "V":
-                nc.vector.tensor_scalar(out=dst, in0=src, scalar1=gw[:, g, t : t + 1], scalar2=None, op0=ALU.mult)
-            else:
-                nc.scalar.activation(out=dst, in_=src, func=ACT.Copy, scale=gw[:, g, t : t + 1])
-
-        def unmix(i, t):
-            w = WIDTHS[i]
-            b = bank("other", [P, w])
-            n = w if w == 512 else P
-            for m0 in range(0, w, n):
-                for g in range(HALVES):
-                    codes, scales = held["xq", i, g]
-                    nc.tensor.matmul_mx(
-                        out=b[:, m0 : m0 + n],
-                        lhsT=uw[:, g, 256 * t : 256 * (t + 1)].bitcast(FP4X4),
-                        lhsT_scale=us[:, g, P * t : P * (t + 1)],
-                        rhs=codes[:, m0 : m0 + n].bitcast(FP8X4),
-                        rhs_scale=scales[:, m0 : m0 + n],
-                        start=(g == 0),
-                        stop=(g == HALVES - 1),
-                    )
-            held["ab", i, t] = b
-
-        def relu(i, t, eng="S"):
-            if t == 0:
-                held["a", i] = work.tile([P, PACK, WIDTHS[i]], BF16, name="a", bufs=1)
-            nc.scalar.activation(out=held["a", i][:, t, :], in_=held["ab", i, t][:], func=ACT.Relu, bias=bias_sb[:, t : t + 1])
-
-        def interleave(dst, src, eng):
-            copier(eng)(
+        def interleave(dst, src):
+            nc.vector.tensor_copy(
                 out=dst.rearrange("p (c i) t -> p c t i", i=4), in_=src.rearrange("p t (c i) -> p c t i", i=4)
             )
 
-        def interleave_a(i, eng="V"):
-            held["ai", i] = work.tile([P, WIDTHS[i], PACK], BF16, name="ai", bufs=1, align_bytes=64)
-            interleave(held["ai", i][:], held["a", i][:], eng)
-
-        def quantise_a(i):
-            codes = work.tile([P, WIDTHS[i]], U32, name="aq", align_bytes=64)
-            scales = work.tile([P, WIDTHS[i]], U8, name="asc", align_bytes=64)
-            nc.vector.quantize_mx(
-                out=codes[:].bitcast(FP8X4), scales=scales[:], in_=held["ai", i][:].rearrange("p m t -> p (m t)")
+        def turn_x(h, pair):
+            group, g = divmod(h, G)
+            b = bank("other", [P, 2, 2, P])
+            for jj in range(2):
+                words = x_sb[TILES * group + 2 * pair + jj, g].bitcast(F32)
+                for u in range(2):
+                    nc.tensor.transpose(b[:, jj, u, :], words[:, u::2], ident[:])
+            if pair == 0:
+                held["xt", h] = work.tile([P, WIDTH, PACK], BF16, name="xt%d" % g, align_bytes=64, bufs=3)
+            turned = held["xt", h][:].rearrange("p m t -> p (m t)").bitcast(F32)
+            nc.scalar.copy(
+                out=turned[:, 512 * pair : 512 * (pair + 1)].rearrange("p (j m u) -> p j m u", j=2, u=2),
+                in_=b[:].rearrange("p j u m -> p j m u"),
             )
-            held["aq", i] = (codes, scales)
 
-        def rebuild(i, g, t):
-            b = bank("fit", [P, WIDTHS[i]])
-            codes, scales = held["aq", i]
+        def quantise_x(h):
+            codes = work.tile([P, WIDTH], U32, name="xq%d" % (h % G), align_bytes=64)
+            scales = work.tile([P, WIDTH], U8, name="xs%d" % (h % G), align_bytes=64)
+            quantise(codes[:], scales[:], held["xt", h][:])
+            held["xq", h] = (codes, scales)
+
+        def scale_x(on_vector):
+            h, t = divmod(used["slices"], PACK)
+            used["slices"] = used["slices"] + 1
+            if t == 0:
+                held["y", h] = work.tile([P, PACK, WIDTH], F32, name="y%d" % (h % G))
+            dst = held["y", h][:, t, :]
+            src = held["xt", h][:, :, t]
+            factor = gain_weight[:, h % G, t : t + 1]
+            if on_vector:
+                nc.vector.tensor_scalar(out=dst, in0=src, scalar1=factor, scalar2=None, op0=ALU.mult)
+            else:
+                nc.scalar.activation(out=dst, in_=src, func=ACT.Copy, scale=factor)
+
+        def unmix(group, t, on_vector=False):
+            b = bank("other", [P, WIDTH])
+            for g in range(G):
+                codes, scales = held["xq", G * group + g]
+                nc.tensor.matmul_mx(
+                    out=b[:],
+                    lhsT=uw[:, g, 2 * P * t : 2 * P * (t + 1)].bitcast(FP4X4),
+                    lhsT_scale=us[:, g, P * t : P * (t + 1)],
+                    rhs=codes[:].bitcast(FP8X4),
+                    rhs_scale=scales[:],
+                    start=(g == 0),
+                    stop=(g == G - 1),
+                )
+            if t == 0:
+                held["a", group] = work.tile([P, PACK, WIDTH], BF16, name="a", bufs=1)
+            dst = held["a", group][:, t, :]
+            shift = bias_sb[:, t : t + 1]
+            if on_vector:
+                nc.vector.tensor_scalar(out=dst, in0=b[:], scalar1=shift, scalar2=0.0, op0=ALU.add, op1=ALU.max)
+            else:
+                nc.scalar.activation(out=dst, in_=b[:], func=ACT.Relu, bias=shift)
+
+        def interleave_a(group):
+            held["ai", group] = work.tile([P, WIDTH, PACK], BF16, name="ai", bufs=1, align_bytes=64)
+            interleave(held["ai", group][:], held["a", group][:])
+
+        def quantise_a(group):
+            codes = work.tile([P, WIDTH], U32, name="aq", align_bytes=64)
+            scales = work.tile([P, WIDTH], U8, name="asc", align_bytes=64)
+            quantise(codes[:], scales[:], held["ai", group][:])
+            held["aq", group] = (codes, scales)
+
+        def rebuild(h, t):
+            group, g = divmod(h, G)
+            b = bank("fit", [P, WIDTH])
+            codes, scales = held["aq", group]
             nc.tensor.matmul_mx(
                 out=b[:],
-                lhsT=dw[:, g, 256 * t : 256 * (t + 1)].bitcast(FP4X4),
+                lhsT=dw[:, g, 2 * P * t : 2 * P * (t + 1)].bitcast(FP4X4),
                 lhsT_scale=ds[:, g, P * t : P * (t + 1)],
                 rhs=codes[:].bitcast(FP8X4),
                 rhs_scale=scales[:],
                 start=True,
                 stop=True,
             )
-            held["fb", i, g, t] = b
+            held["fit", h, t] = b
 
-        def residual(i, g, t, m0=0, m1=512):
-            y = held["y", i, g][:, t, m0:m1]
+        def residual(h, t, m0, m1):
+            y = held["y", h][:, t, m0:m1]
             nc.vector.scalar_tensor_tensor(
-                out=y, in0=held["fb", i, g, t][:, m0:m1], scalar=neg_w[:, g, t : t + 1], in1=y, op0=ALU.mult, op1=ALU.add
+                out=y,
+                in0=held["fit", h, t][:, m0:m1],
+                scalar=neg_weight[:, h % G, t : t + 1],
+                in1=y,
+                op0=ALU.mult,
+                op1=ALU.add,
             )
 
-        def turn_y(i, g, j):
+        def turn_y(h, j):
             b = bank("other", [P, PACK, P])
             for t in range(PACK):
-                nc.tensor.transpose(b[:, t, :], held["y", i, g][:, t, P * j : P * (j + 1)], ident[:])
-            held["yb", i, g, j] = b
-
-        def copy_y(i, g, j, eng="S"):
-            if j == 0:
-                held["yo", i, g] = work.tile([P, tiles(i), K_PASS], F32, name="yo", bufs=3)
-            copier(eng)(
-                out=held["yo", i, g][:, j, :].rearrange("m (p t) -> m p t", t=PACK),
-                in_=held["yb", i, g, j][:].rearrange("m t p -> m p t"),
+                nc.tensor.transpose(b[:, t, :], held["y", h][:, t, P * j : P * (j + 1)], ident[:])
+            if j % 2 == 0:
+                held["yo", h, j // 2] = work.tile([P, 2, K_PASS], F32, name="yo", bufs=6)
+            nc.scalar.copy(
+                out=held["yo", h, j // 2][:, j % 2, :].rearrange("m (p t) -> m p t", t=PACK),
+                in_=b[:].rearrange("m t p -> m p t"),
             )
 
-        def store_y(i, g, j0, j1):
-            rows = out_0[starts[i] : starts[i] + WIDTHS[i], K_PASS * g : K_PASS * (g + 1)].rearrange("(j m) b -> m j b", m=P)
-            nc.sync.dma_start(out=rows[:, j0:j1, :], in_=held["yo", i, g][:, j0:j1, :])
+        def store_y(h, j0, j1):
+            group, g = divmod(h, G)
+            rows = out_0[WIDTH * group : WIDTH * (group + 1), K_PASS * g : K_PASS * (g + 1)]
+            nc.sync.dma_start(
+                out=rows.rearrange("(j m) b -> m j b", m=P)[:, j0:j1, :],
+                in_=held["yo", h, j0 // 2][:, j0 % 2 : j0 % 2 + j1 - j0, :],
+            )
 
-        def round_y(i, g, m0, m1, eng="V"):
-            if ("yi", i, g) not in held:
-                held["yi", i, g] = work.tile([P, WIDTHS[i], PACK], BF16, name="yi", align_bytes=64, bufs=YI_BUFS)
-            dst = held["yi", i, g][:, m0:m1, :]
-            src = held["y", i, g][:, :, m0:m1]
-            if eng == "G":
+        def round_y(h, m0, m1, on_gpsimd=False):
+            if m0 == 0:
+                name = "yi" if h < HALVES - 1 else "yi_last"
+                held["yi", h] = work.tile([P, WIDTH, PACK], BF16, name=name, align_bytes=64, bufs=1)
+            dst = held["yi", h][:, m0:m1, :]
+            src = held["y", h][:, :, m0:m1]
+            if on_gpsimd:
                 nc.gpsimd.tensor_scalar(
                     out=dst, in0=src.rearrange("p t m -> p m t"), scalar1=1.0, scalar2=1.0, op0=ALU.mult, op1=ALU.mult
                 )
             else:
-                interleave(dst, src, eng)
+                interleave(dst, src)
 
-        def quantise_y(i, g, m0=0, m1=512):
-            cols = slice(starts[i] + m0, starts[i] + m1)
-            nc.vector.quantize_mx(
-                out=y_codes[:, g, cols].bitcast(FP8X4),
-                scales=y_scales[:, g, cols],
-                in_=held["yi", i, g][:, m0:m1, :].rearrange("p m t -> p (m t)"),
-            )
+        def quantise_y(h):
+            group, g = divmod(h, G)
+            cols = slice(WIDTH * group, WIDTH * (group + 1))
+            scales = ys_last[:, g, :] if group == GROUPS - 1 else ys_main[:, g, cols]
+            quantise(y_codes[:, g, cols], scales, held["yi", h][:])
             words = out_1[g].rearrange("p m t -> p (m t)").bitcast(I32)
             nc.sync.dma_start(out=words[:, cols], in_=y_codes[:, g, cols].bitcast(I32))
 
-        def store_scales(m0, m1):
+        def store_scales(queue, plane, m0, m1):
             rows = out_2.rearrange("g q m -> q g m")
             for q in range(4):
-                nc.sync.dma_start(
-                    out=rows[4 * q : 4 * q + 4, :, m0:m1].bitcast(I32),
-                    in_=y_scales[32 * q : 32 * q + 4, :, m0:m1].bitcast(I32),
+                queue.dma_start(
+                    out=rows[4 * q : 4 * q + 4, :, m0:m1].bitcast(I32), in_=plane[32 * q : 32 * q + 4].bitcast(I32)
                 )
 
-        def scale_some(i, g, ts, eng):
-            for t in ts:
-                scale_x(i, g, t, eng)
-
+        used["slices"] = 0
         nc.vector.memset(us_raw[:].rearrange("p g n -> p (g n)").bitcast(I32), 0)
         nc.vector.memset(ds_raw[:].rearrange("p g n -> p (g n)").bitcast(I32), 0)
         make_identity(nc, ident[:])
         load_x(0, 2, 0, 1)
         nc.scalar.dma_start(out=weight_sb[:], in_=weight.rearrange("(g p t) -> p g t", p=P, t=PACK))
-        load_x(2, 4, 0, 1)
         nc.sync.dma_start(out=uw_raw[:].bitcast(I32), in_=u_words.rearrange("g p n -> p g n").bitcast(I32))
-        load_scales(nc.scalar, us_raw, u_scales.rearrange("g q n -> q g n"))
+        load_x(2, 4, 0, 1)
         load_x(0, 4, 1, 2)
+        load_scales(us_raw, u_scales.rearrange("g q n -> q g n"))
         nc.sync.dma_start(out=gain_sb[:], in_=gain.rearrange("(g p t) -> p g t", p=P, t=PACK))
-        nc.sync.dma_start(
-            out=dw_raw[:].rearrange("p g n -> p (g n)").bitcast(I32), in_=d_words[0].bitcast(I32)
-        )
-        load_scales(nc.gpsimd, ds_raw, d_scales[0].rearrange("q (g n) -> q g n", g=HALVES))
+        load_x(4, 8, 0, 1)
         nc.sync.dma_start(out=bias_sb[:], in_=bias.rearrange("(p t) -> p t", t=PACK))
-        load_x(4, 8)
-        for j0 in range(8, PIXELS // P, 4):
-            load_x(j0, j0 + 4)
-        nc.scalar.activation(out=neg_w[:], in_=weight_sb[:], func=ACT.Copy, scale=-1.0)
+        nc.sync.dma_start(out=dw_raw[:].rearrange("p g n -> p (g n)").bitcast(I32), in_=d_words[0].bitcast(I32))
+        load_scales(ds_raw, d_scales[0].rearrange("q (g n) -> q g n", g=G))
+        load_x(4, 8, 1, 2)
+        load_x(8, 12, 0, 1)
+        load_x(8, 12, 1, 2)
+        load_x(12, 16, 0, 2)
+        nc.scalar.activation(out=neg_weight[:], in_=weight_sb[:], func=ACT.Copy, scale=-1.0)
 
-        def turn_and_copy_x(i, g):
-            for pair in range(pairs(i)):
-                turn_x(i, g, pair)
-                copy_x(i, g, pair)
-
-        def unmix_all(i):
-            for t in range(PACK):
-                unmix(i, t)
-                relu(i, t)
-
-        turn_and_copy_x(0, 0)
-        turn_and_copy_x(0, 1)
-        for g in range(HALVES):
-            permute_words(uw, uw_raw, g)
-        quantise_x(0, 0)
-        permute_scales(us, us_raw)
-        nc.vector.tensor_tensor(out=gw[:], in0=gain_sb[:], in1=weight_sb[:], op=ALU.mult)
-        quantise_x(0, 1)
-        scale_some(0, 0, range(HEAD_S), "S")
-        unmix_all(0)
-        for g in range(HALVES):
-            permute_words(dw, dw_raw, g)
-        permute_scales(ds, ds_raw)
-        scale_some(0, 0, range(HEAD_S, PACK), "V")
-        turn_and_copy_x(1, 0)
-        turn_and_copy_x(1, 1)
-        scale_some(0, 1, range(HEAD_V), "V")
+        for g in range(G):
+            reorder_words(uw, uw_raw, g)
+        nc.vector.tensor_tensor(out=gain_weight[:], in0=gain_sb[:], in1=weight_sb[:], op=ALU.mult)
+        for h in (0, 1):
+            for pair in range(2):
+                turn_x(h, pair)
+        scale_x(True)
+        quantise_x(0)
+        reorder_scales(us, us_raw)
+        scale_x(False)
+        quantise_x(1)
+        scale_x(True)
+        for g in range(G):
+            reorder_words(dw, dw_raw, g)
+        scale_x(False)
+        reorder_scales(ds, ds_raw)
+        turn_x(2, 0)
+        unmix(0, 0)
+        turn_x(2, 1)
+        quantise_x(2)
+        for t in range(1, PACK):
+            unmix(0, t)
+        scale_x(True)
+        scale_x(True)
+        turn_x(3, 0)
         interleave_a(0)
-        quantise_x(1, 0)
+        turn_x(3, 1)
+        quantise_x(3)
+        scale_x(False)
         quantise_a(0)
-        quantise_x(1, 1)
-        scale_some(0, 1, range(HEAD_V, PACK), "S")
-        for t in range(PACK):
-            rebuild(0, 0, t)
-
-        halves = HALVES * groups
+        turn_x(4, 0)
+        turn_x(4, 1)
+        scale_x(False)
+        unmix(1, 0)
+        quantise_x(4)
+        rebuild(0, 0)
+        unmix(1, 1)
+        for t in range(1, PACK):
+            rebuild(0, t)
 
         def step(h):
-            i, g = divmod(h, HALVES)
-            n = i + 1
-            last = h == halves - 1
-            on_v = D_ON_V[h]
-            early = D_EARLY[h]
-            before = divmod(h - 1, HALVES)
-            cut = G_COLS[h - 1] if h >= 1 else 0
-            if h >= 2 and G_COLS[h - 2]:
-                quantise_y(*divmod(h - 2, HALVES))
+            group, second = divmod(h + UNMIX_AHEAD, G)
+            unmixing = group < GROUPS
+            turning = h + TURN_AHEAD < HALVES
+            cut = ROUND_ON_GPSIMD[h]
             if cut:
-                round_y(*before, 0, cut, "G")
-            if h >= 1 and E_ON_S[h - 1]:
-                round_y(*before, 0, E_ON_S[h - 1], "S")
-            if g == 0 and n < groups:
-                unmix_all(n)
-            if g == 1 and n + 1 < groups:
-                turn_and_copy_x(n + 1, 0)
-                turn_and_copy_x(n + 1, 1)
-            if last:
-                for m0 in (0, 256):
-                    for t in range(PACK):
-                        residual(i, g, t, m0, m0 + 256)
-                    if m0 == 0:
-                        if cut and cut < 512:
-                            round_y(*before, cut, 512)
-                        if not cut:
-                            quantise_y(*before)
-                    for j in (m0 // P, m0 // P + 1):
-                        turn_y(i, g, j)
-                        copy_y(i, g, j)
-                        store_y(i, g, j, j + 1)
-                round_y(i, g, 0, 256)
-                if cut:
-                    quantise_y(*before)
-                round_y(i, g, 256, 512)
-                quantise_y(i, g)
-                store_scales(starts[i], PIXELS)
-                return
-            for t in range(PACK):
-                residual(i, g, t)
-            if cut and cut < 512:
-                round_y(*before, cut, 512)
-            if h >= 1 and not cut:
-                quantise_y(*before)
-            if h == halves - 2:
-                store_scales(0, starts[i])
-            if n < groups:
-                scale_some(n, g, range(on_v, on_v + early), "S")
-            s_cols = E_ON_S[h]
-            for t in range(FIT_EARLY[h]):
-                rebuild(*divmod(h + 1, HALVES), t)
-            for j in range(tiles(i)):
-                turn_y(i, g, j)
-                if j == 1:
-                    for t in range(FIT_EARLY[h], PACK):
-                        rebuild(*divmod(h + 1, HALVES), t)
-                copy_y(i, g, j)
+                round_y(h - 1, 0, cut, on_gpsimd=True)
+            for t in range(PACK - 1):
+                residual(h, t, 0, WIDTH)
+            if unmixing:
+                unmix(group, 2 * second, on_vector=h in RELU_ON_VECTOR)
+            residual(h, PACK - 1, 0, WIDTH)
+            if h > 0 and cut < WIDTH:
+                round_y(h - 1, cut, WIDTH)
+            if unmixing:
+                unmix(group, 2 * second + 1)
+            if turning:
+                turn_x(h + TURN_AHEAD, 0)
+                turn_x(h + TURN_AHEAD, 1)
+            for n in range(SCALE_ON_VECTOR[h]):
+                scale_x(True)
+            if unmixing and second:
+                interleave_a(group)
+            if turning:
+                quantise_x(h + TURN_AHEAD)
+            if h > 0:
+                quantise_y(h - 1)
+            if h - 1 == G * (GROUPS - 1) - 1:
+                store_scales(nc.sync, ys_main, 0, main_pixels)
+            for n in range(min(SCALE_ON_SCALAR[h], SCALE_BEFORE_TURN)):
+                scale_x(False)
+            rebuild(h + 1, 0)
+            rebuild(h + 1, 1)
+            for j in range(TILES):
+                turn_y(h, j)
                 if j % 2:
-                    store_y(i, g, j - 1, j + 1)
-            if n < groups:
-                scale_some(n, g, range(on_v + early, PACK), "S")
-            if not G_COLS[h] and s_cols < 512:
-                round_y(i, g, s_cols, 512)
-            if g == 0 and n < groups:
-                interleave_a(n)
-            if g == 1 and n + 1 < groups:
-                quantise_x(n + 1, 0)
-            if n < groups:
-                scale_some(n, g, range(on_v), "V")
-            if g == 0 and n < groups:
-                quantise_a(n)
-            if g == 1 and n + 1 < groups:
-                quantise_x(n + 1, 1)
+                    store_y(h, j - 1, j + 1)
+            rebuild(h + 1, 2)
+            rebuild(h + 1, 3)
+            for n in range(SCALE_BEFORE_TURN, SCALE_ON_SCALAR[h]):
+                scale_x(False)
+            if unmixing and second:
+                quantise_a(group)
 
-        for h in range(halves):
+        for h in range(HALVES - 1):
             step(h)
+
+        last = HALVES - 1
+        mid = WIDTH // 2
+        round_y(last - 1, 0, WIDTH, on_gpsimd=True)
+        for t in range(PACK):
+            residual(last, t, 0, mid)
+        turn_y(last, 0)
+        turn_y(last, 1)
+        store_y(last, 0, 2)
+        for t in range(PACK):
+            residual(last, t, mid, WIDTH)
+        round_y(last, 0, mid)
+        for j in (2, 3):
+            turn_y(last, j)
+            store_y(last, j, j + 1)
+        round_y(last, mid, WIDTH)
+        quantise_y(last - 1)
+        quantise_y(last)
+        store_scales(nc.scalar, ys_last, main_pixels, PIXELS)

@@ -225,7 +225,12 @@ def tile_unmixing_residual_planes_h1_kernel(
             src = held["y", h][:, :, m0:m1]
             if on_gpsimd:
                 nc.gpsimd.tensor_scalar(
-                    out=dst, in0=src.rearrange("p t m -> p m t"), scalar1=1.0, scalar2=1.0, op0=ALU.mult, op1=ALU.mult
+                    out=dst.rearrange("p (c i) t -> p c t i", i=2),
+                    in0=src.rearrange("p t (c i) -> p c t i", i=2),
+                    scalar1=1.0,
+                    scalar2=1.0,
+                    op0=ALU.mult,
+                    op1=ALU.mult,
                 )
             else:
                 interleave(dst, src)

from contextlib import ExitStack

import concourse.mybir as mybir
from concourse.masks import make_identity

PIXELS, BANDS, MEMBERS = 2048, 1024, 512
FLOPS = 2 * 2 * PIXELS * BANDS * MEMBERS

F32 = mybir.dt.float32
BF16 = mybir.dt.bfloat16
U32 = mybir.dt.uint32
I32 = mybir.dt.int32
U8 = mybir.dt.uint8
FP8X4 = mybir.dt.float8_e4m3fn_x4
FP4X4 = mybir.dt.float4_e2m1fn_x4
ALU = mybir.AluOpType
ACT = mybir.ActivationFunctionType

P = 128
PACK = 4
K_PASS = P * PACK
G = BANDS // K_PASS
WIDTH = 512
TILES = WIDTH // P
GROUPS = PIXELS // WIDTH
HALVES = G * GROUPS
RING = 4
TURN_AHEAD = 5
UNMIX_AHEAD = 3

RELU_ON_VECTOR = (2, 4)
SCALE_ON_VECTOR = [2, 1, 2, 1, 0, 1, 1]
SCALE_ON_SCALAR = [1, 2, 3, 1, 4, 4, 1]
ROUND_ON_GPSIMD = [0, 0, 512, 384, 512, 384, 384]
SCALE_BEFORE_TURN = 3


def tile_unmixing_residual_planes_h1_kernel(
    tc, x, u_words, u_scales, bias, d_words, d_scales, gain, weight, out_0, out_1, out_2
):
    nc = tc.nc

    with ExitStack() as ctx:
        keep = ctx.enter_context(tc.tile_pool(name="keep", bufs=1))
        work = ctx.enter_context(tc.tile_pool(name="work", bufs=2))
        psum = ctx.enter_context(tc.psum_pool(name="psum", bufs=1))
        ctx.enter_context(tc.manual_schedule())

        uw_raw = keep.tile([P, G, 2 * K_PASS], U8, name="uw_raw")
        dw_raw = keep.tile([P, G, 2 * K_PASS], U8, name="dw_raw")
        us_raw = keep.tile([P, G, K_PASS], U8, name="us_raw")
        ds_raw = keep.tile([P, G, K_PASS], U8, name="ds_raw")
        uw = keep.tile([P, G, 2 * K_PASS], U8, name="uw", align_bytes=64)
        dw = keep.tile([P, G, 2 * K_PASS], U8, name="dw", align_bytes=64)
        us = keep.tile([P, G, K_PASS], U8, name="us", align_bytes=64)
        ds = keep.tile([P, G, K_PASS], U8, name="ds", align_bytes=64)
        bias_sb = keep.tile([P, PACK], BF16, name="bias_sb")
        gain_sb = keep.tile([P, G, PACK], BF16, name="gain_sb")
        weight_sb = keep.tile([P, G, PACK], BF16, name="weight_sb")
        gain_weight = keep.tile([P, G, PACK], F32, name="gain_weight")
        neg_weight = keep.tile([P, G, PACK], F32, name="neg_weight")
        ident = keep.tile([P, P], F32, name="ident")
        main_pixels = PIXELS - WIDTH
        y_codes = keep.tile([P, G, PIXELS], U32, name="y_codes", align_bytes=64)
        ys_main = keep.tile([P, G, main_pixels], U8, name="ys_main", align_bytes=64)
        ys_last = keep.tile([P, G, WIDTH], U8, name="ys_last", align_bytes=64)

        x_rows = x.rearrange("(j p) b -> p j b", p=P)
        x_sb = {}
        held = {}
        used = {"fit": 0, "other": 0}

        def bank(ring, shape):
            tag = "%s%d" % (ring, used[ring] % RING)
            used[ring] = used[ring] + 1
            return psum.tile(shape, F32, name=tag, tag=tag)

        def load_x(j0, j1, g0, g1):
            part = keep.tile([P, j1 - j0, K_PASS * (g1 - g0)], BF16, name="x_%d_%d" % (j0, g0))
            nc.sync.dma_start(out=part[:], in_=x_rows[:, j0:j1, K_PASS * g0 : K_PASS * g1])
            for j in range(j0, j1):
                for g in range(g0, g1):
                    x_sb[j, g] = part[:, j - j0, K_PASS * (g - g0) : K_PASS * (g - g0 + 1)]

        def load_scales(raw, rows):
            for q in range(4):
                nc.sync.dma_start(out=raw[32 * q : 32 * q + 4].bitcast(I32), in_=rows[4 * q : 4 * q + 4].bitcast(I32))

        def reorder_words(dst, raw, g):
            nc.vector.tensor_copy(
                out=dst[:, g, :].rearrange("p (t m b) -> p t m b", t=PACK, b=2),
                in_=raw[:, g, :].rearrange("p (m t b) -> p t m b", t=PACK, b=2),
            )

        def reorder_scales(dst, raw):
            nc.vector.tensor_copy(
                out=dst[:].rearrange("p g (t m) -> p g t m", t=PACK),
                in_=raw[:].rearrange("p g (m t) -> p g t m", t=PACK),
            )

        def quantise(codes, scales, values):
            nc.vector.quantize_mx(out=codes.bitcast(FP8X4), scales=scales, in_=values.rearrange("p m t -> p (m t)"))

        def interleave(dst, src):
            nc.vector.tensor_copy(
                out=dst.rearrange("p (c i) t -> p c t i", i=4), in_=src.rearrange("p t (c i) -> p c t i", i=4)
            )

        def turn_x(h, pair):
            group, g = divmod(h, G)
            b = bank("other", [P, 2, 2, P])
            for jj in range(2):
                words = x_sb[TILES * group + 2 * pair + jj, g].bitcast(F32)
                for u in range(2):
                    nc.tensor.transpose(b[:, jj, u, :], words[:, u::2], ident[:])
            if pair == 0:
                held["xt", h] = work.tile([P, WIDTH, PACK], BF16, name="xt%d" % g, align_bytes=64, bufs=3)
            turned = held["xt", h][:].rearrange("p m t -> p (m t)").bitcast(F32)
            nc.scalar.copy(
                out=turned[:, 512 * pair : 512 * (pair + 1)].rearrange("p (j m u) -> p j m u", j=2, u=2),
                in_=b[:].rearrange("p j u m -> p j m u"),
            )

        def quantise_x(h):
            codes = work.tile([P, WIDTH], U32, name="xq%d" % (h % G), align_bytes=64)
            scales = work.tile([P, WIDTH], U8, name="xs%d" % (h % G), align_bytes=64)
            quantise(codes[:], scales[:], held["xt", h][:])
            held["xq", h] = (codes, scales)

        def scale_x(on_vector):
            h, t = divmod(used["slices"], PACK)
            used["slices"] = used["slices"] + 1
            if t == 0:
                held["y", h] = work.tile([P, PACK, WIDTH], F32, name="y%d" % (h % G))
            dst = held["y", h][:, t, :]
            src = held["xt", h][:, :, t]
            factor = gain_weight[:, h % G, t : t + 1]
            if on_vector:
                nc.vector.tensor_scalar(out=dst, in0=src, scalar1=factor, scalar2=None, op0=ALU.mult)
            else:
                nc.scalar.activation(out=dst, in_=src, func=ACT.Copy, scale=factor)

        def unmix(group, t, on_vector=False):
            b = bank("other", [P, WIDTH])
            for g in range(G):
                codes, scales = held["xq", G * group + g]
                nc.tensor.matmul_mx(
                    out=b[:],
                    lhsT=uw[:, g, 2 * P * t : 2 * P * (t + 1)].bitcast(FP4X4),
                    lhsT_scale=us[:, g, P * t : P * (t + 1)],
                    rhs=codes[:].bitcast(FP8X4),
                    rhs_scale=scales[:],
                    start=(g == 0),
                    stop=(g == G - 1),
                )
            if t == 0:
                held["a", group] = work.tile([P, PACK, WIDTH], BF16, name="a", bufs=1)
            dst = held["a", group][:, t, :]
            shift = bias_sb[:, t : t + 1]
            if on_vector:
                nc.vector.tensor_scalar(out=dst, in0=b[:], scalar1=shift, scalar2=0.0, op0=ALU.add, op1=ALU.max)
            else:
                nc.scalar.activation(out=dst, in_=b[:], func=ACT.Relu, bias=shift)

        def interleave_a(group):
            held["ai", group] = work.tile([P, WIDTH, PACK], BF16, name="ai", bufs=1, align_bytes=64)
            interleave(held["ai", group][:], held["a", group][:])

        def quantise_a(group):
            codes = work.tile([P, WIDTH], U32, name="aq", align_bytes=64)
            scales = work.tile([P, WIDTH], U8, name="asc", align_bytes=64)
            quantise(codes[:], scales[:], held["ai", group][:])
            held["aq", group] = (codes, scales)

        def rebuild(h, t):
            group, g = divmod(h, G)
            b = bank("fit", [P, WIDTH])
            codes, scales = held["aq", group]
            nc.tensor.matmul_mx(
                out=b[:],
                lhsT=dw[:, g, 2 * P * t : 2 * P * (t + 1)].bitcast(FP4X4),
                lhsT_scale=ds[:, g, P * t : P * (t + 1)],
                rhs=codes[:].bitcast(FP8X4),
                rhs_scale=scales[:],
                start=True,
                stop=True,
            )
            held["fit", h, t] = b

        def residual(h, t, m0, m1):
            y = held["y", h][:, t, m0:m1]
            nc.vector.scalar_tensor_tensor(
                out=y,
                in0=held["fit", h, t][:, m0:m1],
                scalar=neg_weight[:, h % G, t : t + 1],
                in1=y,
                op0=ALU.mult,
                op1=ALU.add,
            )

        def turn_y(h, j):
            b = bank("other", [P, PACK, P])
            for t in range(PACK):
                nc.tensor.transpose(b[:, t, :], held["y", h][:, t, P * j : P * (j + 1)], ident[:])
            if j % 2 == 0:
                held["yo", h, j // 2] = work.tile([P, 2, K_PASS], F32, name="yo", bufs=6)
            nc.scalar.copy(
                out=held["yo", h, j // 2][:, j % 2, :].rearrange("m (p t) -> m p t", t=PACK),
                in_=b[:].rearrange("m t p -> m p t"),
            )

        def store_y(h, j0, j1):
            group, g = divmod(h, G)
            rows = out_0[WIDTH * group : WIDTH * (group + 1), K_PASS * g : K_PASS * (g + 1)]
            nc.sync.dma_start(
                out=rows.rearrange("(j m) b -> m j b", m=P)[:, j0:j1, :],
                in_=held["yo", h, j0 // 2][:, j0 % 2 : j0 % 2 + j1 - j0, :],
            )

        def round_y(h, m0, m1, on_gpsimd=False):
            if m0 == 0:
                name = "yi" if h < HALVES - 1 else "yi_last"
                held["yi", h] = work.tile([P, WIDTH, PACK], BF16, name=name, align_bytes=64, bufs=1)
            dst = held["yi", h][:, m0:m1, :]
            src = held["y", h][:, :, m0:m1]
            if on_gpsimd:
                nc.gpsimd.tensor_scalar(
                    out=dst.rearrange("p (c i) t -> p c t i", i=2),
                    in0=src.rearrange("p t (c i) -> p c t i", i=2),
                    scalar1=1.0,
                    scalar2=1.0,
                    op0=ALU.mult,
                    op1=ALU.mult,
                )
            else:
                interleave(dst, src)

        def quantise_y(h):
            group, g = divmod(h, G)
            cols = slice(WIDTH * group, WIDTH * (group + 1))
            scales = ys_last[:, g, :] if group == GROUPS - 1 else ys_main[:, g, cols]
            quantise(y_codes[:, g, cols], scales, held["yi", h][:])
            words = out_1[g].rearrange("p m t -> p (m t)").bitcast(I32)
            nc.sync.dma_start(out=words[:, cols], in_=y_codes[:, g, cols].bitcast(I32))

        def store_scales(queue, plane, m0, m1):
            rows = out_2.rearrange("g q m -> q g m")
            for q in range(4):
                queue.dma_start(
                    out=rows[4 * q : 4 * q + 4, :, m0:m1].bitcast(I32), in_=plane[32 * q : 32 * q + 4].bitcast(I32)
                )

        used["slices"] = 0
        nc.vector.memset(us_raw[:].rearrange("p g n -> p (g n)").bitcast(I32), 0)
        nc.vector.memset(ds_raw[:].rearrange("p g n -> p (g n)").bitcast(I32), 0)
        make_identity(nc, ident[:])
        load_x(0, 2, 0, 1)
        nc.scalar.dma_start(out=weight_sb[:], in_=weight.rearrange("(g p t) -> p g t", p=P, t=PACK))
        nc.sync.dma_start(out=uw_raw[:].bitcast(I32), in_=u_words.rearrange("g p n -> p g n").bitcast(I32))
        load_x(2, 4, 0, 1)
        load_x(0, 4, 1, 2)
        load_scales(us_raw, u_scales.rearrange("g q n -> q g n"))
        nc.sync.dma_start(out=gain_sb[:], in_=gain.rearrange("(g p t) -> p g t", p=P, t=PACK))
        load_x(4, 8, 0, 1)
        nc.sync.dma_start(out=bias_sb[:], in_=bias.rearrange("(p t) -> p t", t=PACK))
        nc.sync.dma_start(out=dw_raw[:].rearrange("p g n -> p (g n)").bitcast(I32), in_=d_words[0].bitcast(I32))
        load_scales(ds_raw, d_scales[0].rearrange("q (g n) -> q g n", g=G))
        load_x(4, 8, 1, 2)
        load_x(8, 12, 0, 1)
        load_x(8, 12, 1, 2)
        load_x(12, 16, 0, 2)
        nc.scalar.activation(out=neg_weight[:], in_=weight_sb[:], func=ACT.Copy, scale=-1.0)

        for g in range(G):
            reorder_words(uw, uw_raw, g)
        nc.vector.tensor_tensor(out=gain_weight[:], in0=gain_sb[:], in1=weight_sb[:], op=ALU.mult)
        for h in (0, 1):
            for pair in range(2):
                turn_x(h, pair)
        scale_x(True)
        quantise_x(0)
        reorder_scales(us, us_raw)
        scale_x(False)
        quantise_x(1)
        scale_x(True)
        for g in range(G):
            reorder_words(dw, dw_raw, g)
        scale_x(False)
        reorder_scales(ds, ds_raw)
        turn_x(2, 0)
        unmix(0, 0)
        turn_x(2, 1)
        quantise_x(2)
        for t in range(1, PACK):
            unmix(0, t)
        scale_x(True)
        scale_x(True)
        turn_x(3, 0)
        interleave_a(0)
        turn_x(3, 1)
        quantise_x(3)
        scale_x(False)
        quantise_a(0)
        turn_x(4, 0)
        turn_x(4, 1)
        scale_x(False)
        unmix(1, 0)
        quantise_x(4)
        rebuild(0, 0)
        unmix(1, 1)
        for t in range(1, PACK):
            rebuild(0, t)

        def step(h):
            group, second = divmod(h + UNMIX_AHEAD, G)
            unmixing = group < GROUPS
            turning = h + TURN_AHEAD < HALVES
            cut = ROUND_ON_GPSIMD[h]
            if cut:
                round_y(h - 1, 0, cut, on_gpsimd=True)
            for t in range(PACK - 1):
                residual(h, t, 0, WIDTH)
            if unmixing:
                unmix(group, 2 * second, on_vector=h in RELU_ON_VECTOR)
            residual(h, PACK - 1, 0, WIDTH)
            if h > 0 and cut < WIDTH:
                round_y(h - 1, cut, WIDTH)
            if unmixing:
                unmix(group, 2 * second + 1)
            if turning:
                turn_x(h + TURN_AHEAD, 0)
                turn_x(h + TURN_AHEAD, 1)
            for n in range(SCALE_ON_VECTOR[h]):
                scale_x(True)
            if unmixing and second:
                interleave_a(group)
            if turning:
                quantise_x(h + TURN_AHEAD)
            if h > 0:
                quantise_y(h - 1)
            if h - 1 == G * (GROUPS - 1) - 1:
                store_scales(nc.sync, ys_main, 0, main_pixels)
            for n in range(min(SCALE_ON_SCALAR[h], SCALE_BEFORE_TURN)):
                scale_x(False)
            rebuild(h + 1, 0)
            rebuild(h + 1, 1)
            for j in range(TILES):
                turn_y(h, j)
                if j % 2:
                    store_y(h, j - 1, j + 1)
            rebuild(h + 1, 2)
            rebuild(h + 1, 3)
            for n in range(SCALE_BEFORE_TURN, SCALE_ON_SCALAR[h]):
                scale_x(False)
            if unmixing and second:
                quantise_a(group)

        for h in range(HALVES - 1):
            step(h)

        last = HALVES - 1
        mid = WIDTH // 2
        round_y(last - 1, 0, WIDTH, on_gpsimd=True)
        for t in range(PACK):
            residual(last, t, 0, mid)
        turn_y(last, 0)
        turn_y(last, 1)
        store_y(last, 0, 2)
        for t in range(PACK):
            residual(last, t, mid, WIDTH)
        round_y(last, 0, mid)
        for j in (2, 3):
            turn_y(last, j)
            store_y(last, j, j + 1)
        round_y(last, mid, WIDTH)
        quantise_y(last - 1)
        quantise_y(last)
        store_scales(nc.scalar, ys_last, main_pixels, PIXELS)
